import numpy as np, ml_dtypes
CORES = [15,47,79,175,207]
N = 5
import mx_ref
NC, G = 128, 2
C, C2 = np.float32(0.041), np.float32(0.01834)
BF = ml_dtypes.bfloat16
def cut(t, i, w=512):
    return t[:, w * i:w * i + w]
def tile(rs):
    return np.stack(rs, axis=2).reshape(128, -1).astype(BF)
def layer(w, X):
    out = []
    for i in range(G):
        for t in range(len(X)):
            p = mx_ref.matmul(mx_ref.quantize(cut(w, len(X) * i + t)), X[t])
            z = p if t == 0 else z + p
        out.append(z)
    return out
def act(Z):
    return [np.maximum(s * z, 0) * C for z in Z for s in (1, -1)]
def act2(Z):
    return [np.maximum(s * z, 0) * C2 for z in Z for s in (1, -1)]
def setup_inputs(rng):
    def f(*shape):
        return mx_ref.flush((rng.standard_normal(shape, dtype=np.float32) * np.exp2(rng.integers(-2, 3, shape[:-1] + (1,)))).astype(BF))
    return {"x": f(N, 128, 4 * NC), "w1": f(N, 128, G * 512), "w2": f(N, 128, G * 512), "w3": f(N, 128, G * 512), "w4": f(N, 128, 512)}
def setup_inputs_blocks(rng):
    d = setup_inputs(rng)
    for k in ("x", "w1", "w2", "w3", "w4"): d[k] = mx_ref.spread(d[k], rng, 2)
    return d
def setup_inputs_wide(rng):
    d = setup_inputs(rng)
    for k in ("x", "w1", "w2", "w3", "w4"): d[k] = mx_ref.flush((d[k].astype(np.float32) * np.exp2(rng.integers(-4, 5, (N, 1, 1))).astype(np.float32)).astype(BF))
    return d
def reference(x, w1, w2, w3, w4, own=None):
    X = [mx_ref.quantize(x[j]) for j in range(N)]
    t = np.stack([np.stack([tile(act(layer(w1[r], [X[c]]))) for c in range(N)]) for r in range(N)])
    uset = t if own is None else own["t"]
    h = np.zeros((N, 128, 4 * NC), BF)
    for c in range(N):
        for r in range(N):
            P = layer(w2[r], [mx_ref.quantize(uset[r][c])])
            Z = P if r == 0 else [z + p for z, p in zip(Z, P)]
        h[c] = tile(act2(Z))
    use = h if own is None else own["h"]
    H = [mx_ref.quantize(use[j]) for j in range(N)]
    y = np.zeros((N, 128, NC), np.float32)
    for c in range(N):
        for r in range(N):
            p = mx_ref.matmul(mx_ref.quantize(w4[r]), mx_ref.quantize(tile(act(layer(w3[r], [H[c]])))))
            y[c] = p if r == 0 else y[c] + p
    return {"t": t, "h": h, "y": y}

@@ -1,0 +1,279 @@
+import numpy as np
+from concourse.bass import DstId, RemoteDMATransfer
+from concourse.mybir import dt, AluOpType, ActivationFunctionType
+
+N, NC, G = 5, 128, 2
+C1 = float(np.float32(0.041))
+C2 = float(np.float32(0.01834))
+CORES_ALL = 256
+W34 = 3 * NC
+CARRY = [[1, 2], [3, 4]]
+FOLD = 0
+FOLDED = [1, 2, 3]
+
+_F8, _U8, _BF, _F32 = "float8_e4m3fn_x4", "uint8", "bfloat16", "float32"
+SCRATCH = {
+    "xb": ("sbuf", [128, 512], _BF), "wb": ("sbuf", [128, 7 * 512], _BF),
+    "xq": ("sbuf", [128, N * NC], _F8), "xs": ("sbuf", [128, N * NC], _U8),
+    "wq": ("sbuf", [128, 7 * NC], _F8), "ws": ("sbuf", [128, 7 * NC], _U8),
+    "tb": ("sbuf", [128, N * 512], _BF),
+    "tq": ("sbuf", [128, N * NC], _F8), "ts": ("sbuf", [128, N * NC], _U8),
+    "so": ("sbuf", [128, N * 256], _F32), "sl": ("sbuf", [128, 256], _F32), "sa": ("sbuf", [128, 2 * 256], _F32),
+    "fl": ("sbuf", [128, N * 256], _F32), "fa": ("sbuf", [128, 3 * 256], _F32), "fs": ("sbuf", [128, 256], _F32),
+    "hb": ("sbuf", [128, 512], _BF),
+    "hq": ("sbuf", [128, NC], _F8), "hs": ("sbuf", [128, NC], _U8),
+    "pq": ("sbuf", [128, N * W34], _F8), "ps": ("sbuf", [128, N * W34], _U8),
+    "rq": ("sbuf", [128, W34], _F8), "rs": ("sbuf", [128, W34], _U8),
+    "ub": ("sbuf", [128, N * 512], _BF),
+    "uq": ("sbuf", [128, N * NC], _F8), "us": ("sbuf", [128, N * NC], _U8),
+    "ya": ("sbuf", [128, NC], _F32),
+    "pm": ("psum", [128, 8 * 512], _F32),
+}
+SEMAPHORES = (
+    ["lx", "lw1", "lw2", "lw3", "lw4", "qx", "qw1", "qw2", "qw34", "own"]
+    + ["%s%d" % (n, k) for n in ("za", "zb", "ac", "tq", "pa", "pb", "cp", "va", "vb", "uc", "uq", "ls") for k in range(N)]
+    + ["%s%d" % (n, k) for n in ("ax", "aw", "af", "fa") for k in range(N)]
+    + ["as", "afs", "sa", "s0", "s1", "hc", "hq", "rw", "yd", "yc"]
+    + ["leftx", "leftw", "leftf", "st"]
+)
+
+
+def _engines(m):
+    return [e for e in range(16) if m >> e & 1]
+
+
+def _bits(es):
+    return sum(1 << e for e in es)
+
+
+def _helpers(topo, core, dst):
+    return [h for h in range(CORES_ALL) if (topo.host(h), topo.chip(h)) == (topo.host(core), topo.chip(core))
+            and topo.die(h) != topo.die(core) and topo.may_write(core, h) and topo.may_write(h, dst)][:len(CARRY)]
+
+
+def _copy(topo, core, dests, mask, sem, dst, src):
+    ids = []
+    for d in dests:
+        rid, pid = topo.addr(d, core)
+        ids.append(DstId(rid=rid, pnc=pid))
+    return RemoteDMATransfer(dst_ids=ids, dma_engine_mask=mask, remote_sem=sem, srcs=[src], dsts=[dst] * len(ids), alu_op=0)
+
+
+def _codes(t, a, n=NC):
+    return t[:, a:a + n].bitcast(dt.uint8)
+
+
+def _cols(t, a, n=NC):
+    return t[:, a:a + n]
+
+
+def _inner(topo, core, helper, off):
+    return [e for e in _engines(topo.mask(core, helper)) if not off >> e & 1]
+
+
+def _helper_program(g, r, i, core, T, topo):
+    S, cores = T.sem, T.cores
+    own = cores[r]
+    dests = [cores[(r + k) % N] for k in CARRY[i]]
+    off = topo.mask(core, dests[0])
+    ne = len(_engines(off))
+    g.wait_ge(S["rw"], 2 * len(_inner(topo, own, core, topo.mask(own, dests[0]))))
+    g.remote_dma_fused([_copy(topo, core, dests, off, S["aw%d" % r], _codes(T.pq, r * W34, W34), _codes(T.rq, 0, W34))], local_sem=S["leftw"])
+    g.remote_dma_fused([_copy(topo, core, dests, off, S["aw%d" % r], _cols(T.ps, r * W34, W34), _cols(T.rs, 0, W34))], local_sem=S["leftw"])
+    if i == FOLD:
+        v = g.vector
+        land = [T.fl[:, 256 * ((r + k) % N):256 * ((r + k) % N) + 256] for k in FOLDED]
+        arrived = [S["af%d" % ((r + k) % N)] for k in FOLDED]
+        cur = land[0]
+        v.wait_ge(arrived[0], ne)
+        for j in range(1, len(land)):
+            v.wait_ge(arrived[j], ne)
+            if j > 1:
+                v.wait_ge(S["fa%d" % (j - 1)], 1)
+            nxt = T.fa[:, 256 * j:256 * j + 256]
+            v.tensor_tensor(nxt, cur, land[j], AluOpType.add).then_inc(S["fa%d" % j], 1)
+            cur = nxt
+        rid, pid = topo.addr(own, core)
+        g.wait_ge(S["fa%d" % (len(land) - 1)], 1)
+        g.remote_dma(T.fs[:], cur, S["afs"], S["leftf"], pid, rid, off)
+        g.wait_ge(S["leftf"], ne)
+    g.wait_ge(S["leftw"], 2 * ne)
+
+
+def rank_program(g, core, T, topo):
+    cores = T.cores
+    rank = T.rank_of(core)
+    if rank is None:
+        for r in range(N):
+            hs = _helpers(topo, cores[r], cores[(r + 1) % N])
+            if core in hs:
+                _helper_program(g, r, hs.index(core), core, T, topo)
+        return
+
+    S = T.sem
+    r = rank
+    act, relu, copy = g.scalar.activation, ActivationFunctionType.Relu, ActivationFunctionType.Copy
+    mult, vmax, add = AluOpType.mult, AluOpType.max, AluOpType.add
+    to = [(r + k) % N for k in range(N)]
+    fr = [(r - k) % N for k in range(N)]
+    helpers = _helpers(topo, core, cores[to[1]])
+    off = topo.mask(core, cores[to[1]])
+    ne = len(_engines(off))
+    inner = _inner(topo, core, helpers[0], off)
+
+    def bank(b, n=NC):
+        return T.pm[:, 512 * b:512 * b + n]
+
+    def mm(b, w, wsc, wi, x, xsc, xi, start=True, stop=True):
+        return g.tensor.matmul_mx(bank(b), _cols(w, wi * NC), _cols(wsc, wi * NC), _cols(x, xi * NC), _cols(xsc, xi * NC), start, stop)
+
+    g.sync.dma_start(T.xb[:], T.x[:]).then_inc(S["lx"], 16)
+    g.sync.dma_start(T.wb[:, 0:1024], T.w1[:]).then_inc(S["lw1"], 16)
+    g.sync.dma_start(T.wb[:, 1024:2048], T.w2[:]).then_inc(S["lw2"], 16)
+    g.sync.dma_start(T.wb[:, 2048:3072], T.w3[:]).then_inc(S["lw3"], 16)
+    g.sync.dma_start(T.wb[:, 3072:3584], T.w4[:]).then_inc(S["lw4"], 16)
+
+    q = g.tensor
+    zbank = [0, 2, 0, 2, 0]
+    vbank = [0, 2, 4, 0, 2]
+
+    def z(k):
+        if k:
+            q.wait_ge(S["ax%d" % fr[k]], 2 * ne)
+        for i, n in enumerate(("za", "zb")):
+            mm(zbank[k] + i, T.wq, T.ws, i, T.xq, T.xs, fr[k]).then_inc(S[n + str(k)], 1)
+
+    def p(k):
+        if k == 0:
+            q.wait_ge(S["qw2"], 1)
+        q.wait_ge(S["tq%d" % k], 1)
+        if k > 1:
+            q.wait_ge(S["cp%d" % (k - 1)], 2)
+        for i, n in enumerate(("pa", "pb")):
+            mm((4 if k else 6) + i, T.wq, T.ws, 2 + i, T.tq, T.ts, k).then_inc(S[n + str(k) if k else "own"], 1)
+
+    def vz(k):
+        if k == 0:
+            q.wait_ge(S["qw34"], 2)
+        else:
+            q.wait_ge(S["aw%d" % fr[k]], 2 * ne)
+        if k == 2:
+            q.wait_ge(S["cp%d" % (N - 1)], 2)
+        for i, n in enumerate(("va", "vb")):
+            w = (T.pq, T.ps, 3 * fr[k] + i) if k else (T.wq, T.ws, 4 + i)
+            mm(vbank[k] + i, *w, T.hq, T.hs, 0).then_inc(S[n + str(k)], 1)
+
+    def y(k):
+        q.wait_ge(S["uq%d" % k], 1)
+        w = (T.pq, T.ps, 3 * fr[k] + 2) if k else (T.wq, T.ws, 6)
+        m = mm(6, *w, T.uq, T.us, k, k == 0, k == N - 1)
+        if k == N - 1:
+            m.then_inc(S["yd"], 1)
+
+    q.wait_ge(S["qx"], 1)
+    q.wait_ge(S["qw1"], 1)
+    for f, k in ((z, 0), (p, 0), (z, 1), (p, 1), (z, 2), (p, 2), (z, 3), (z, 4), (p, 3), (p, 4)):
+        f(k)
+    q.wait_ge(S["hq"], 1)
+    for f, k in ((vz, 0), (vz, 1), (vz, 2), (y, 0), (vz, 3), (y, 1), (vz, 4), (y, 2), (y, 3), (y, 4)):
+        f(k)
+
+    s = g.scalar
+
+    def half0(src, tile, k, c, wait, done):
+        s.wait_ge(wait, 1)
+        for b in (0, 1):
+            act(tile[:, 512 * k + b:512 * k + 512:4], src, relu, scale=(c, -c)[b]).then_inc(done, 1)
+
+    for k in range(N):
+        half0(bank(zbank[k]), T.tb, k, C1, S["za%d" % k], S["ac%d" % k])
+        if k:
+            s.wait_ge(S["pa%d" % k], 1)
+            act(T.so[:, 256 * k:256 * k + 128], bank(4), copy).then_inc(S["cp%d" % k], 1)
+    half0(T.sa[:, 256:384], T.hb, 0, C2, S["s0"], S["hc"])
+    for k in range(N):
+        half0(bank(vbank[k]), T.ub, k, C1, S["va%d" % k], S["uc%d" % k])
+    s.wait_ge(S["yd"], 1)
+    act(T.ya[:], bank(6), copy).then_inc(S["yc"], 1)
+
+    v = g.vector
+
+    def half1(src, tile, k, c, wait, done):
+        v.wait_ge(wait, 1)
+        for b in (2, 3):
+            v.tensor_scalar(tile[:, 512 * k + b:512 * k + 512:4], src, (c, -c)[b - 2], 0.0, mult, vmax).then_inc(done, 1)
+
+    def quant(codes, planes, i, tile, k, done, sem):
+        v.wait_ge(done, 4)
+        v.quantize_mx(_cols(codes, i * NC), _cols(planes, i * NC), tile[:, 512 * k:512 * k + 512]).then_inc(sem, 1)
+
+    def qweights(a, n, load, sem):
+        v.wait_ge(load, 16)
+        v.quantize_mx(_cols(T.wq, a * NC, n * NC), _cols(T.ws, a * NC, n * NC), T.wb[:, 512 * a:512 * (a + n)]).then_inc(sem, 1)
+
+    v.wait_ge(S["lx"], 16)
+    v.quantize_mx(_cols(T.xq, r * NC), _cols(T.xs, r * NC), T.xb[:]).then_inc(S["qx"], 1)
+    qweights(0, 2, S["lw1"], S["qw1"])
+    qweights(2, 2, S["lw2"], S["qw2"])
+    half1(bank(1), T.tb, 0, C1, S["zb0"], S["ac0"])
+    quant(T.tq, T.ts, 0, T.tb, 0, S["ac0"], S["tq0"])
+    qweights(4, 2, S["lw3"], S["qw34"])
+    qweights(6, 1, S["lw4"], S["qw34"])
+    for k in range(1, N):
+        half1(bank(zbank[k] + 1), T.tb, k, C1, S["zb%d" % k], S["ac%d" % k])
+        quant(T.tq, T.ts, k, T.tb, k, S["ac%d" % k], S["tq%d" % k])
+        v.wait_ge(S["pb%d" % k], 1)
+        v.tensor_copy(T.so[:, 256 * k + 128:256 * k + 256], bank(5)).then_inc(S["cp%d" % k], 1)
+    v.wait_ge(S["own"], 2)
+    v.wait_ge(S["as"], ne)
+    for i in range(G):
+        v.tensor_tensor(T.sa[:, 128 * i:128 * i + 128], bank(6 + i), T.sl[:, 128 * i:128 * i + 128], add).then_inc(S["sa"], 1)
+    v.wait_ge(S["sa"], 2)
+    v.wait_ge(S["afs"], ne)
+    for i in range(G):
+        a = 128 * i
+        v.tensor_tensor(T.sa[:, 256 + a:384 + a], T.sa[:, a:a + 128], T.fs[:, a:a + 128], add).then_inc(S["s%d" % i], 1)
+    half1(T.sa[:, 384:512], T.hb, 0, C2, S["s1"], S["hc"])
+    quant(T.hq, T.hs, 0, T.hb, 0, S["hc"], S["hq"])
+    for k in range(N):
+        half1(bank(vbank[k] + 1), T.ub, k, C1, S["vb%d" % k], S["uc%d" % k])
+        quant(T.uq, T.us, k, T.ub, k, S["uc%d" % k], S["uq%d" % k])
+
+    def cast(src, ks):
+        g.remote_dma_fused([_copy(topo, core, [cores[to[k]] for k in ks], off, S["ax%d" % r], src, src)], local_sem=S["leftx"])
+
+    g.wait_ge(S["qx"], 1)
+    cast(_codes(T.xq, r * NC), [1, 2])
+    cast(_cols(T.xs, r * NC), [1, 2, 3, 4])
+    g.wait_ge(S["qw34"], 2)
+    for h in helpers:
+        g.remote_dma_fused([_copy(topo, core, [h], _bits(inner), S["rw"], _codes(T.rq, 0, W34), _codes(T.wq, 4 * NC, W34))], local_sem=S["leftw"])
+        g.remote_dma_fused([_copy(topo, core, [h], _bits(inner), S["rw"], _cols(T.rs, 0, W34), _cols(T.ws, 4 * NC, W34))], local_sem=S["leftw"])
+    cast(_codes(T.xq, r * NC), [3, 4])
+    for k in range(1, N):
+        g.wait_ge(S["cp%d" % k], 2)
+        dst = fr[k]
+        if k in FOLDED:
+            d = _helpers(topo, cores[dst], cores[(dst + 1) % N])[FOLD]
+            land, sem = T.fl[:, 256 * r:256 * r + 256], S["af%d" % r]
+        else:
+            d, land, sem = cores[dst], T.sl[:], S["as"]
+        rid, pid = topo.addr(d, core)
+        g.remote_dma(land, T.so[:, 256 * k:256 * k + 256], sem, S["ls%d" % k], pid, rid, off)
+    g.wait_ge(S["leftw"], 2 * len(helpers) * len(inner))
+
+    def keep(k):
+        g.sync.wait_ge(S["ac%d" % k], 4)
+        g.sync.dma_start(T.t[fr[k]], T.tb[:, 512 * k:512 * k + 512]).then_inc(S["st"], 16)
+
+    g.sync.wait_ge(S["leftx"], 3 * ne)
+    keep(0)
+    for k in range(1, N):
+        g.sync.wait_ge(S["ls%d" % k], ne)
+    for k in range(1, N):
+        keep(k)
+    g.sync.wait_ge(S["hc"], 4)
+    g.sync.dma_start(T.h[:], T.hb[:]).then_inc(S["st"], 16)
+    g.sync.wait_ge(S["yc"], 1)
+    g.sync.dma_start(T.y[:], T.ya[:]).then_inc(S["st"], 16)
+    g.sync.wait_ge(S["st"], 16 * (N + 2))

@@ -7,9 +7,17 @@ C1 = float(np.float32(0.041))
 C2 = float(np.float32(0.01834))
 CORES_ALL = 256
 W34 = 3 * NC
-CARRY = [[1, 2], [3, 4]]
+CARRY = [[1], [2, 3]]
+STRAIGHT = 4
 FOLD = 0
 FOLDED = [1, 2, 3]
+SEND = ["c1", "s1", "c2", "s2", "w0", "c3", "s3", "w1", "c4", "s4"]
+TENSOR1 = ["z0", "p0", "z1", "z2", "p1", "z3", "p2", "p3", "z4", "p4"]
+ACT1 = ["a1", "a2", "c1", "a3", "c2", "c3", "a4", "c4"]
+COPY2 = [1, 2, 3]
+TENSOR2 = ["v0", "v1", "v2", "v3", "y0", "v4", "y1", "y2", "y3", "y4"]
+ACT2 = ["a0", "a1", "q0", "a2", "q1", "a3", "q2", "a4", "q3", "q4"]
+SHARE = [1, 3]
 
 _F8, _U8, _BF, _F32 = "float8_e4m3fn_x4", "uint8", "bfloat16", "float32"
 SCRATCH = {
@@ -19,7 +27,7 @@ SCRATCH = {
     "tb": ("sbuf", [128, N * 512], _BF),
     "tq": ("sbuf", [128, N * NC], _F8), "ts": ("sbuf", [128, N * NC], _U8),
     "so": ("sbuf", [128, N * 256], _F32), "sl": ("sbuf", [128, 256], _F32), "sa": ("sbuf", [128, 2 * 256], _F32),
-    "fl": ("sbuf", [128, N * 256], _F32), "fa": ("sbuf", [128, 3 * 256], _F32), "fs": ("sbuf", [128, 256], _F32),
+    "fl": ("sbuf", [128, N * 256], _F32), "fa": ("sbuf", [128, 2 * 256], _F32), "fs": ("sbuf", [128, 256], _F32),
     "hb": ("sbuf", [128, 512], _BF),
     "hq": ("sbuf", [128, NC], _F8), "hs": ("sbuf", [128, NC], _U8),
     "pq": ("sbuf", [128, N * W34], _F8), "ps": ("sbuf", [128, N * W34], _U8),
@@ -31,10 +39,10 @@ SCRATCH = {
 }
 SEMAPHORES = (
     ["lx", "lw1", "lw2", "lw3", "lw4", "qx", "qw1", "qw2", "qw34", "own"]
-    + ["%s%d" % (n, k) for n in ("za", "zb", "ac", "tq", "pa", "pb", "cp", "va", "vb", "uc", "uq", "ls") for k in range(N)]
-    + ["%s%d" % (n, k) for n in ("ax", "aw", "af", "fa") for k in range(N)]
-    + ["as", "afs", "sa", "s0", "s1", "hc", "hq", "rw", "yd", "yc"]
-    + ["leftx", "leftw", "leftf", "st"]
+    + ["%s%d" % (n, k) for n in ("za", "zb", "ac", "tq", "pa", "pb", "cp", "va", "vb", "uc", "ur", "uq", "ls") for k in range(N)]
+    + ["%s%d" % (n, k) for n in ("ax", "aw", "af") for k in range(N)]
+    + ["as", "afs0", "afs1", "fa", "fh0", "fh1", "sa", "s0", "s1", "hc", "hq", "rw", "yd", "yc"]
+    + ["leftx", "leftw", "leftd", "leftf", "st"]
 )
 
 
@@ -81,22 +89,21 @@ def _helper_program(g, r, i, core, T, topo):
     g.remote_dma_fused([_copy(topo, core, dests, off, S["aw%d" % r], _codes(T.pq, r * W34, W34), _codes(T.rq, 0, W34))], local_sem=S["leftw"])
     g.remote_dma_fused([_copy(topo, core, dests, off, S["aw%d" % r], _cols(T.ps, r * W34, W34), _cols(T.rs, 0, W34))], local_sem=S["leftw"])
     if i == FOLD:
-        v = g.vector
-        land = [T.fl[:, 256 * ((r + k) % N):256 * ((r + k) % N) + 256] for k in FOLDED]
-        arrived = [S["af%d" % ((r + k) % N)] for k in FOLDED]
-        cur = land[0]
-        v.wait_ge(arrived[0], ne)
-        for j in range(1, len(land)):
-            v.wait_ge(arrived[j], ne)
-            if j > 1:
-                v.wait_ge(S["fa%d" % (j - 1)], 1)
-            nxt = T.fa[:, 256 * j:256 * j + 256]
-            v.tensor_tensor(nxt, cur, land[j], AluOpType.add).then_inc(S["fa%d" % j], 1)
-            cur = nxt
+        v, add = g.vector, AluOpType.add
+        src = [(r + k) % N for k in FOLDED]
+        a, b, c = [256 * x for x in src]
+        v.wait_ge(S["af%d" % src[0]], ne)
+        v.wait_ge(S["af%d" % src[1]], ne)
+        v.tensor_tensor(T.fa[:, 0:256], T.fl[:, a:a + 256], T.fl[:, b:b + 256], add).then_inc(S["fa"], 1)
+        v.wait_ge(S["fa"], 1)
+        v.wait_ge(S["af%d" % src[2]], ne)
         rid, pid = topo.addr(own, core)
-        g.wait_ge(S["fa%d" % (len(land) - 1)], 1)
-        g.remote_dma(T.fs[:], cur, S["afs"], S["leftf"], pid, rid, off)
-        g.wait_ge(S["leftf"], ne)
+        for h in range(G):
+            o = 128 * h
+            v.tensor_tensor(T.fa[:, 256 + o:384 + o], T.fa[:, o:o + 128], T.fl[:, c + o:c + o + 128], add).then_inc(S["fh%d" % h], 1)
+            g.wait_ge(S["fh%d" % h], 1)
+            g.remote_dma(T.fs[:, o:o + 128], T.fa[:, 256 + o:384 + o], S["afs%d" % h], S["leftf"], pid, rid, off)
+        g.wait_ge(S["leftf"], G * ne)
     g.wait_ge(S["leftw"], 2 * ne)
 
 
@@ -159,6 +166,10 @@ def rank_program(g, core, T, topo):
             q.wait_ge(S["aw%d" % fr[k]], 2 * ne)
         if k == 2:
             q.wait_ge(S["cp%d" % (N - 1)], 2)
+        if k > 2:
+            q.wait_ge(S["uc%d" % (k - 3)], 3 if k - 3 in SHARE else 4)
+            if k - 3 in SHARE:
+                q.wait_ge(S["ur%d" % (k - 3)], 1)
         for i, n in enumerate(("va", "vb")):
             w = (T.pq, T.ps, 3 * fr[k] + i) if k else (T.wq, T.ws, 4 + i)
             mm(vbank[k] + i, *w, T.hq, T.hs, 0).then_inc(S[n + str(k)], 1)
@@ -172,11 +183,11 @@ def rank_program(g, core, T, topo):
 
     q.wait_ge(S["qx"], 1)
     q.wait_ge(S["qw1"], 1)
-    for f, k in ((z, 0), (p, 0), (z, 1), (p, 1), (z, 2), (p, 2), (z, 3), (z, 4), (p, 3), (p, 4)):
-        f(k)
+    for o in TENSOR1:
+        (z if o[0] == "z" else p)(int(o[1]))
     q.wait_ge(S["hq"], 1)
-    for f, k in ((vz, 0), (vz, 1), (vz, 2), (y, 0), (vz, 3), (y, 1), (vz, 4), (y, 2), (y, 3), (y, 4)):
-        f(k)
+    for o in TENSOR2:
+        (vz if o[0] == "v" else y)(int(o[1]))
 
     s = g.scalar
 
@@ -185,14 +196,25 @@ def rank_program(g, core, T, topo):
         for b in (0, 1):
             act(tile[:, 512 * k + b:512 * k + 512:4], src, relu, scale=(c, -c)[b]).then_inc(done, 1)
 
-    for k in range(N):
-        half0(bank(zbank[k]), T.tb, k, C1, S["za%d" % k], S["ac%d" % k])
-        if k:
+    half0(bank(zbank[0]), T.tb, 0, C1, S["za0"], S["ac0"])
+    for o in ACT1:
+        k = int(o[1])
+        if o[0] == "a":
+            half0(bank(zbank[k]), T.tb, k, C1, S["za%d" % k], S["ac%d" % k])
+        else:
             s.wait_ge(S["pa%d" % k], 1)
             act(T.so[:, 256 * k:256 * k + 128], bank(4), copy).then_inc(S["cp%d" % k], 1)
+            if k in COPY2:
+                s.wait_ge(S["pb%d" % k], 1)
+                act(T.so[:, 256 * k + 128:256 * k + 256], bank(5), copy).then_inc(S["cp%d" % k], 1)
     half0(T.sa[:, 256:384], T.hb, 0, C2, S["s0"], S["hc"])
+    s.wait_ge(S["s1"], 1)
+    act(T.hb[:, 2::4], T.sa[:, 384:512], relu, scale=C2).then_inc(S["hc"], 1)
     for k in range(N):
         half0(bank(vbank[k]), T.ub, k, C1, S["va%d" % k], S["uc%d" % k])
+        if k in SHARE:
+            s.wait_ge(S["ur%d" % k], 1)
+            act(T.ub[:, 512 * k + 2:512 * k + 512:4], bank(vbank[k] + 1), relu, scale=C1).then_inc(S["uc%d" % k], 1)
     s.wait_ge(S["yd"], 1)
     act(T.ya[:], bank(6), copy).then_inc(S["yc"], 1)
 
@@ -203,8 +225,8 @@ def rank_program(g, core, T, topo):
         for b in (2, 3):
             v.tensor_scalar(tile[:, 512 * k + b:512 * k + 512:4], src, (c, -c)[b - 2], 0.0, mult, vmax).then_inc(done, 1)
 
-    def quant(codes, planes, i, tile, k, done, sem):
-        v.wait_ge(done, 4)
+    def quant(codes, planes, i, tile, k, done, sem, n=4):
+        v.wait_ge(done, n)
         v.quantize_mx(_cols(codes, i * NC), _cols(planes, i * NC), tile[:, 512 * k:512 * k + 512]).then_inc(sem, 1)
 
     def qweights(a, n, load, sem):
@@ -219,37 +241,50 @@ def rank_program(g, core, T, topo):
     quant(T.tq, T.ts, 0, T.tb, 0, S["ac0"], S["tq0"])
     qweights(4, 2, S["lw3"], S["qw34"])
     qweights(6, 1, S["lw4"], S["qw34"])
-    for k in range(1, N):
-        half1(bank(zbank[k] + 1), T.tb, k, C1, S["zb%d" % k], S["ac%d" % k])
-        quant(T.tq, T.ts, k, T.tb, k, S["ac%d" % k], S["tq%d" % k])
-        v.wait_ge(S["pb%d" % k], 1)
-        v.tensor_copy(T.so[:, 256 * k + 128:256 * k + 256], bank(5)).then_inc(S["cp%d" % k], 1)
+    for o in ACT1:
+        k = int(o[1])
+        if o[0] == "a":
+            half1(bank(zbank[k] + 1), T.tb, k, C1, S["zb%d" % k], S["ac%d" % k])
+            quant(T.tq, T.ts, k, T.tb, k, S["ac%d" % k], S["tq%d" % k])
+        elif k not in COPY2:
+            v.wait_ge(S["pb%d" % k], 1)
+            v.tensor_copy(T.so[:, 256 * k + 128:256 * k + 256], bank(5)).then_inc(S["cp%d" % k], 1)
     v.wait_ge(S["own"], 2)
     v.wait_ge(S["as"], ne)
     for i in range(G):
         v.tensor_tensor(T.sa[:, 128 * i:128 * i + 128], bank(6 + i), T.sl[:, 128 * i:128 * i + 128], add).then_inc(S["sa"], 1)
     v.wait_ge(S["sa"], 2)
-    v.wait_ge(S["afs"], ne)
     for i in range(G):
         a = 128 * i
+        v.wait_ge(S["afs%d" % i], ne)
         v.tensor_tensor(T.sa[:, 256 + a:384 + a], T.sa[:, a:a + 128], T.fs[:, a:a + 128], add).then_inc(S["s%d" % i], 1)
-    half1(T.sa[:, 384:512], T.hb, 0, C2, S["s1"], S["hc"])
+    v.wait_ge(S["s1"], 1)
+    v.tensor_scalar(T.hb[:, 3::4], T.sa[:, 384:512], -C2, 0.0, mult, vmax).then_inc(S["hc"], 1)
     quant(T.hq, T.hs, 0, T.hb, 0, S["hc"], S["hq"])
-    for k in range(N):
-        half1(bank(vbank[k] + 1), T.ub, k, C1, S["vb%d" % k], S["uc%d" % k])
-        quant(T.uq, T.us, k, T.ub, k, S["uc%d" % k], S["uq%d" % k])
+    for o in ACT2:
+        k = int(o[1])
+        if o[0] == "a" and k in SHARE:
+            v.wait_ge(S["vb%d" % k], 1)
+            v.tensor_scalar(T.ub[:, 512 * k + 3:512 * k + 512:4], bank(vbank[k] + 1), -C1, 0.0, mult, vmax).then_inc(S["ur%d" % k], 1)
+        elif o[0] == "a":
+            half1(bank(vbank[k] + 1), T.ub, k, C1, S["vb%d" % k], S["uc%d" % k])
+        else:
+            if k in SHARE:
+                v.wait_ge(S["ur%d" % k], 1)
+            quant(T.uq, T.us, k, T.ub, k, S["uc%d" % k], S["uq%d" % k], 3 if k in SHARE else 4)
 
-    def cast(src, ks):
-        g.remote_dma_fused([_copy(topo, core, [cores[to[k]] for k in ks], off, S["ax%d" % r], src, src)], local_sem=S["leftx"])
-
+    w34 = (_codes(T.wq, 4 * NC, W34), _cols(T.ws, 4 * NC, W34))
     g.wait_ge(S["qx"], 1)
-    cast(_codes(T.xq, r * NC), [1, 2])
-    cast(_cols(T.xs, r * NC), [1, 2, 3, 4])
-    g.wait_ge(S["qw34"], 2)
-    for h in helpers:
-        g.remote_dma_fused([_copy(topo, core, [h], _bits(inner), S["rw"], _codes(T.rq, 0, W34), _codes(T.wq, 4 * NC, W34))], local_sem=S["leftw"])
-        g.remote_dma_fused([_copy(topo, core, [h], _bits(inner), S["rw"], _cols(T.rs, 0, W34), _cols(T.ws, 4 * NC, W34))], local_sem=S["leftw"])
-    cast(_codes(T.xq, r * NC), [3, 4])
+    for o in SEND:
+        k = int(o[1])
+        if o[0] == "w":
+            if k == 0:
+                g.wait_ge(S["qw34"], 2)
+            for d, f in zip((_codes(T.rq, 0, W34), _cols(T.rs, 0, W34)), w34):
+                g.remote_dma_fused([_copy(topo, core, [helpers[k]], _bits(inner), S["rw"], d, f)], local_sem=S["leftw"])
+        else:
+            f = _codes(T.xq, r * NC) if o[0] == "c" else _cols(T.xs, r * NC)
+            g.remote_dma_fused([_copy(topo, core, [cores[to[k]]], off, S["ax%d" % r], f, f)], local_sem=S["leftx"])
     for k in range(1, N):
         g.wait_ge(S["cp%d" % k], 2)
         dst = fr[k]
@@ -260,18 +295,17 @@ def rank_program(g, core, T, topo):
             d, land, sem = cores[dst], T.sl[:], S["as"]
         rid, pid = topo.addr(d, core)
         g.remote_dma(land, T.so[:, 256 * k:256 * k + 256], sem, S["ls%d" % k], pid, rid, off)
+    for d, f in zip((_codes(T.pq, r * W34, W34), _cols(T.ps, r * W34, W34)), w34):
+        g.remote_dma_fused([_copy(topo, core, [cores[to[STRAIGHT]]], off, S["aw%d" % r], d, f)], local_sem=S["leftd"])
+    g.wait_ge(S["leftx"], 2 * (N - 1) * ne)
     g.wait_ge(S["leftw"], 2 * len(helpers) * len(inner))
+    for k in range(1, N):
+        g.wait_ge(S["ls%d" % k], ne)
 
-    def keep(k):
+    g.sync.wait_ge(S["leftd"], 2 * ne)
+    for k in range(N):
         g.sync.wait_ge(S["ac%d" % k], 4)
         g.sync.dma_start(T.t[fr[k]], T.tb[:, 512 * k:512 * k + 512]).then_inc(S["st"], 16)
-
-    g.sync.wait_ge(S["leftx"], 3 * ne)
-    keep(0)
-    for k in range(1, N):
-        g.sync.wait_ge(S["ls%d" % k], ne)
-    for k in range(1, N):
-        keep(k)
     g.sync.wait_ge(S["hc"], 4)
     g.sync.dma_start(T.h[:], T.hb[:]).then_inc(S["st"], 16)
     g.sync.wait_ge(S["yc"], 1)

import numpy as np
from concourse.bass import DstId, RemoteDMATransfer
from concourse.mybir import dt, AluOpType, ActivationFunctionType

N, NC, G = 5, 128, 2
C1 = float(np.float32(0.041))
C2 = float(np.float32(0.01834))
CORES_ALL = 256
W34 = 3 * NC
CARRY = [[1], [2, 3]]
STRAIGHT = 4
FOLD = 0
FOLDED = [1, 2, 3]
SEND = ["c1", "s1", "c2", "s2", "w0", "c3", "s3", "w1", "c4", "s4"]
TENSOR1 = ["z0", "p0", "z1", "z2", "p1", "z3", "p2", "p3", "z4", "p4"]
ACT1 = ["a1", "a2", "c1", "a3", "c2", "c3", "a4", "c4"]
COPY2 = [1, 2, 3]
TENSOR2 = ["v0", "v1", "v2", "v3", "y0", "v4", "y1", "y2", "y3", "y4"]
ACT2 = ["a0", "a1", "q0", "a2", "q1", "a3", "q2", "a4", "q3", "q4"]
SHARE = [1, 3]

_F8, _U8, _BF, _F32 = "float8_e4m3fn_x4", "uint8", "bfloat16", "float32"
SCRATCH = {
    "xb": ("sbuf", [128, 512], _BF), "wb": ("sbuf", [128, 7 * 512], _BF),
    "xq": ("sbuf", [128, N * NC], _F8), "xs": ("sbuf", [128, N * NC], _U8),
    "wq": ("sbuf", [128, 7 * NC], _F8), "ws": ("sbuf", [128, 7 * NC], _U8),
    "tb": ("sbuf", [128, N * 512], _BF),
    "tq": ("sbuf", [128, N * NC], _F8), "ts": ("sbuf", [128, N * NC], _U8),
    "so": ("sbuf", [128, N * 256], _F32), "sl": ("sbuf", [128, 256], _F32), "sa": ("sbuf", [128, 2 * 256], _F32),
    "fl": ("sbuf", [128, N * 256], _F32), "fa": ("sbuf", [128, 2 * 256], _F32), "fs": ("sbuf", [128, 256], _F32),
    "hb": ("sbuf", [128, 512], _BF),
    "hq": ("sbuf", [128, NC], _F8), "hs": ("sbuf", [128, NC], _U8),
    "pq": ("sbuf", [128, N * W34], _F8), "ps": ("sbuf", [128, N * W34], _U8),
    "rq": ("sbuf", [128, W34], _F8), "rs": ("sbuf", [128, W34], _U8),
    "ub": ("sbuf", [128, N * 512], _BF),
    "uq": ("sbuf", [128, N * NC], _F8), "us": ("sbuf", [128, N * NC], _U8),
    "ya": ("sbuf", [128, NC], _F32),
    "pm": ("psum", [128, 8 * 512], _F32),
}
SEMAPHORES = (
    ["lx", "lw1", "lw2", "lw3", "lw4", "qx", "qw1", "qw2", "qw34", "own"]
    + ["%s%d" % (n, k) for n in ("za", "zb", "ac", "tq", "pa", "pb", "cp", "va", "vb", "uc", "ur", "uq", "ls") for k in range(N)]
    + ["%s%d" % (n, k) for n in ("ax", "aw", "af") for k in range(N)]
    + ["as", "afs0", "afs1", "fa", "fh0", "fh1", "sa", "s0", "s1", "hc", "hq", "rw", "yd", "yc"]
    + ["leftx", "leftw", "leftd", "leftf", "st"]
)


def _engines(m):
    return [e for e in range(16) if m >> e & 1]


def _bits(es):
    return sum(1 << e for e in es)


def _helpers(topo, core, dst):
    return [h for h in range(CORES_ALL) if (topo.host(h), topo.chip(h)) == (topo.host(core), topo.chip(core))
            and topo.die(h) != topo.die(core) and topo.may_write(core, h) and topo.may_write(h, dst)][:len(CARRY)]


def _copy(topo, core, dests, mask, sem, dst, src):
    ids = []
    for d in dests:
        rid, pid = topo.addr(d, core)
        ids.append(DstId(rid=rid, pnc=pid))
    return RemoteDMATransfer(dst_ids=ids, dma_engine_mask=mask, remote_sem=sem, srcs=[src], dsts=[dst] * len(ids), alu_op=0)


def _codes(t, a, n=NC):
    return t[:, a:a + n].bitcast(dt.uint8)


def _cols(t, a, n=NC):
    return t[:, a:a + n]


def _inner(topo, core, helper, off):
    return [e for e in _engines(topo.mask(core, helper)) if not off >> e & 1]


def _helper_program(g, r, i, core, T, topo):
    S, cores = T.sem, T.cores
    own = cores[r]
    dests = [cores[(r + k) % N] for k in CARRY[i]]
    off = topo.mask(core, dests[0])
    ne = len(_engines(off))
    g.wait_ge(S["rw"], 2 * len(_inner(topo, own, core, topo.mask(own, dests[0]))))
    g.remote_dma_fused([_copy(topo, core, dests, off, S["aw%d" % r], _codes(T.pq, r * W34, W34), _codes(T.rq, 0, W34))], local_sem=S["leftw"])
    g.remote_dma_fused([_copy(topo, core, dests, off, S["aw%d" % r], _cols(T.ps, r * W34, W34), _cols(T.rs, 0, W34))], local_sem=S["leftw"])
    if i == FOLD:
        v, add = g.vector, AluOpType.add
        src = [(r + k) % N for k in FOLDED]
        a, b, c = [256 * x for x in src]
        v.wait_ge(S["af%d" % src[0]], ne)
        v.wait_ge(S["af%d" % src[1]], ne)
        v.tensor_tensor(T.fa[:, 0:256], T.fl[:, a:a + 256], T.fl[:, b:b + 256], add).then_inc(S["fa"], 1)
        v.wait_ge(S["fa"], 1)
        v.wait_ge(S["af%d" % src[2]], ne)
        rid, pid = topo.addr(own, core)
        for h in range(G):
            o = 128 * h
            v.tensor_tensor(T.fa[:, 256 + o:384 + o], T.fa[:, o:o + 128], T.fl[:, c + o:c + o + 128], add).then_inc(S["fh%d" % h], 1)
            g.wait_ge(S["fh%d" % h], 1)
            g.remote_dma(T.fs[:, o:o + 128], T.fa[:, 256 + o:384 + o], S["afs%d" % h], S["leftf"], pid, rid, off)
        g.wait_ge(S["leftf"], G * ne)
    g.wait_ge(S["leftw"], 2 * ne)


def rank_program(g, core, T, topo):
    cores = T.cores
    rank = T.rank_of(core)
    if rank is None:
        for r in range(N):
            hs = _helpers(topo, cores[r], cores[(r + 1) % N])
            if core in hs:
                _helper_program(g, r, hs.index(core), core, T, topo)
        return

    S = T.sem
    r = rank
    act, relu, copy = g.scalar.activation, ActivationFunctionType.Relu, ActivationFunctionType.Copy
    mult, vmax, add = AluOpType.mult, AluOpType.max, AluOpType.add
    to = [(r + k) % N for k in range(N)]
    fr = [(r - k) % N for k in range(N)]
    helpers = _helpers(topo, core, cores[to[1]])
    off = topo.mask(core, cores[to[1]])
    ne = len(_engines(off))
    inner = _inner(topo, core, helpers[0], off)

    def bank(b, n=NC):
        return T.pm[:, 512 * b:512 * b + n]

    def mm(b, w, wsc, wi, x, xsc, xi, start=True, stop=True):
        return g.tensor.matmul_mx(bank(b), _cols(w, wi * NC), _cols(wsc, wi * NC), _cols(x, xi * NC), _cols(xsc, xi * NC), start, stop)

    g.sync.dma_start(T.xb[:], T.x[:]).then_inc(S["lx"], 16)
    g.sync.dma_start(T.wb[:, 0:1024], T.w1[:]).then_inc(S["lw1"], 16)
    g.sync.dma_start(T.wb[:, 1024:2048], T.w2[:]).then_inc(S["lw2"], 16)
    g.sync.dma_start(T.wb[:, 2048:3072], T.w3[:]).then_inc(S["lw3"], 16)
    g.sync.dma_start(T.wb[:, 3072:3584], T.w4[:]).then_inc(S["lw4"], 16)

    q = g.tensor
    zbank = [0, 2, 0, 2, 0]
    vbank = [0, 2, 4, 0, 2]

    def z(k):
        if k:
            q.wait_ge(S["ax%d" % fr[k]], 2 * ne)
        for i, n in enumerate(("za", "zb")):
            mm(zbank[k] + i, T.wq, T.ws, i, T.xq, T.xs, fr[k]).then_inc(S[n + str(k)], 1)

    def p(k):
        if k == 0:
            q.wait_ge(S["qw2"], 1)
        q.wait_ge(S["tq%d" % k], 1)
        if k > 1:
            q.wait_ge(S["cp%d" % (k - 1)], 2)
        for i, n in enumerate(("pa", "pb")):
            mm((4 if k else 6) + i, T.wq, T.ws, 2 + i, T.tq, T.ts, k).then_inc(S[n + str(k) if k else "own"], 1)

    def vz(k):
        if k == 0:
            q.wait_ge(S["qw34"], 2)
        else:
            q.wait_ge(S["aw%d" % fr[k]], 2 * ne)
        if k == 2:
            q.wait_ge(S["cp%d" % (N - 1)], 2)
        if k > 2:
            q.wait_ge(S["uc%d" % (k - 3)], 3 if k - 3 in SHARE else 4)
            if k - 3 in SHARE:
                q.wait_ge(S["ur%d" % (k - 3)], 1)
        for i, n in enumerate(("va", "vb")):
            w = (T.pq, T.ps, 3 * fr[k] + i) if k else (T.wq, T.ws, 4 + i)
            mm(vbank[k] + i, *w, T.hq, T.hs, 0).then_inc(S[n + str(k)], 1)

    def y(k):
        q.wait_ge(S["uq%d" % k], 1)
        w = (T.pq, T.ps, 3 * fr[k] + 2) if k else (T.wq, T.ws, 6)
        m = mm(6, *w, T.uq, T.us, k, k == 0, k == N - 1)
        if k == N - 1:
            m.then_inc(S["yd"], 1)

    q.wait_ge(S["qx"], 1)
    q.wait_ge(S["qw1"], 1)
    for o in TENSOR1:
        (z if o[0] == "z" else p)(int(o[1]))
    q.wait_ge(S["hq"], 1)
    for o in TENSOR2:
        (vz if o[0] == "v" else y)(int(o[1]))

    s = g.scalar

    def half0(src, tile, k, c, wait, done):
        s.wait_ge(wait, 1)
        for b in (0, 1):
            act(tile[:, 512 * k + b:512 * k + 512:4], src, relu, scale=(c, -c)[b]).then_inc(done, 1)

    half0(bank(zbank[0]), T.tb, 0, C1, S["za0"], S["ac0"])
    for o in ACT1:
        k = int(o[1])
        if o[0] == "a":
            half0(bank(zbank[k]), T.tb, k, C1, S["za%d" % k], S["ac%d" % k])
        else:
            s.wait_ge(S["pa%d" % k], 1)
            act(T.so[:, 256 * k:256 * k + 128], bank(4), copy).then_inc(S["cp%d" % k], 1)
            if k in COPY2:
                s.wait_ge(S["pb%d" % k], 1)
                act(T.so[:, 256 * k + 128:256 * k + 256], bank(5), copy).then_inc(S["cp%d" % k], 1)
    half0(T.sa[:, 256:384], T.hb, 0, C2, S["s0"], S["hc"])
    s.wait_ge(S["s1"], 1)
    act(T.hb[:, 2::4], T.sa[:, 384:512], relu, scale=C2).then_inc(S["hc"], 1)
    for k in range(N):
        half0(bank(vbank[k]), T.ub, k, C1, S["va%d" % k], S["uc%d" % k])
        if k in SHARE:
            s.wait_ge(S["ur%d" % k], 1)
            act(T.ub[:, 512 * k + 2:512 * k + 512:4], bank(vbank[k] + 1), relu, scale=C1).then_inc(S["uc%d" % k], 1)
    s.wait_ge(S["yd"], 1)
    act(T.ya[:], bank(6), copy).then_inc(S["yc"], 1)

    v = g.vector

    def half1(src, tile, k, c, wait, done):
        v.wait_ge(wait, 1)
        for b in (2, 3):
            v.tensor_scalar(tile[:, 512 * k + b:512 * k + 512:4], src, (c, -c)[b - 2], 0.0, mult, vmax).then_inc(done, 1)

    def quant(codes, planes, i, tile, k, done, sem, n=4):
        v.wait_ge(done, n)
        v.quantize_mx(_cols(codes, i * NC), _cols(planes, i * NC), tile[:, 512 * k:512 * k + 512]).then_inc(sem, 1)

    def qweights(a, n, load, sem):
        v.wait_ge(load, 16)
        v.quantize_mx(_cols(T.wq, a * NC, n * NC), _cols(T.ws, a * NC, n * NC), T.wb[:, 512 * a:512 * (a + n)]).then_inc(sem, 1)

    v.wait_ge(S["lx"], 16)
    v.quantize_mx(_cols(T.xq, r * NC), _cols(T.xs, r * NC), T.xb[:]).then_inc(S["qx"], 1)
    qweights(0, 2, S["lw1"], S["qw1"])
    qweights(2, 2, S["lw2"], S["qw2"])
    half1(bank(1), T.tb, 0, C1, S["zb0"], S["ac0"])
    quant(T.tq, T.ts, 0, T.tb, 0, S["ac0"], S["tq0"])
    qweights(4, 2, S["lw3"], S["qw34"])
    qweights(6, 1, S["lw4"], S["qw34"])
    for o in ACT1:
        k = int(o[1])
        if o[0] == "a":
            half1(bank(zbank[k] + 1), T.tb, k, C1, S["zb%d" % k], S["ac%d" % k])
            quant(T.tq, T.ts, k, T.tb, k, S["ac%d" % k], S["tq%d" % k])
        elif k not in COPY2:
            v.wait_ge(S["pb%d" % k], 1)
            v.tensor_copy(T.so[:, 256 * k + 128:256 * k + 256], bank(5)).then_inc(S["cp%d" % k], 1)
    v.wait_ge(S["own"], 2)
    v.wait_ge(S["as"], ne)
    for i in range(G):
        v.tensor_tensor(T.sa[:, 128 * i:128 * i + 128], bank(6 + i), T.sl[:, 128 * i:128 * i + 128], add).then_inc(S["sa"], 1)
    v.wait_ge(S["sa"], 2)
    for i in range(G):
        a = 128 * i
        v.wait_ge(S["afs%d" % i], ne)
        v.tensor_tensor(T.sa[:, 256 + a:384 + a], T.sa[:, a:a + 128], T.fs[:, a:a + 128], add).then_inc(S["s%d" % i], 1)
    v.wait_ge(S["s1"], 1)
    v.tensor_scalar(T.hb[:, 3::4], T.sa[:, 384:512], -C2, 0.0, mult, vmax).then_inc(S["hc"], 1)
    quant(T.hq, T.hs, 0, T.hb, 0, S["hc"], S["hq"])
    for o in ACT2:
        k = int(o[1])
        if o[0] == "a" and k in SHARE:
            v.wait_ge(S["vb%d" % k], 1)
            v.tensor_scalar(T.ub[:, 512 * k + 3:512 * k + 512:4], bank(vbank[k] + 1), -C1, 0.0, mult, vmax).then_inc(S["ur%d" % k], 1)
        elif o[0] == "a":
            half1(bank(vbank[k] + 1), T.ub, k, C1, S["vb%d" % k], S["uc%d" % k])
        else:
            if k in SHARE:
                v.wait_ge(S["ur%d" % k], 1)
            quant(T.uq, T.us, k, T.ub, k, S["uc%d" % k], S["uq%d" % k], 3 if k in SHARE else 4)

    w34 = (_codes(T.wq, 4 * NC, W34), _cols(T.ws, 4 * NC, W34))
    g.wait_ge(S["qx"], 1)
    for o in SEND:
        k = int(o[1])
        if o[0] == "w":
            if k == 0:
                g.wait_ge(S["qw34"], 2)
            for d, f in zip((_codes(T.rq, 0, W34), _cols(T.rs, 0, W34)), w34):
                g.remote_dma_fused([_copy(topo, core, [helpers[k]], _bits(inner), S["rw"], d, f)], local_sem=S["leftw"])
        else:
            f = _codes(T.xq, r * NC) if o[0] == "c" else _cols(T.xs, r * NC)
            g.remote_dma_fused([_copy(topo, core, [cores[to[k]]], off, S["ax%d" % r], f, f)], local_sem=S["leftx"])
    for k in range(1, N):
        g.wait_ge(S["cp%d" % k], 2)
        dst = fr[k]
        if k in FOLDED:
            d = _helpers(topo, cores[dst], cores[(dst + 1) % N])[FOLD]
            land, sem = T.fl[:, 256 * r:256 * r + 256], S["af%d" % r]
        else:
            d, land, sem = cores[dst], T.sl[:], S["as"]
        rid, pid = topo.addr(d, core)
        g.remote_dma(land, T.so[:, 256 * k:256 * k + 256], sem, S["ls%d" % k], pid, rid, off)
    for d, f in zip((_codes(T.pq, r * W34, W34), _cols(T.ps, r * W34, W34)), w34):
        g.remote_dma_fused([_copy(topo, core, [cores[to[STRAIGHT]]], off, S["aw%d" % r], d, f)], local_sem=S["leftd"])
    g.wait_ge(S["leftx"], 2 * (N - 1) * ne)
    g.wait_ge(S["leftw"], 2 * len(helpers) * len(inner))
    for k in range(1, N):
        g.wait_ge(S["ls%d" % k], ne)

    g.sync.wait_ge(S["leftd"], 2 * ne)
    for k in range(N):
        g.sync.wait_ge(S["ac%d" % k], 4)
        g.sync.dma_start(T.t[fr[k]], T.tb[:, 512 * k:512 * k + 512]).then_inc(S["st"], 16)
    g.sync.wait_ge(S["hc"], 4)
    g.sync.dma_start(T.h[:], T.hb[:]).then_inc(S["st"], 16)
    g.sync.wait_ge(S["yc"], 1)
    g.sync.dma_start(T.y[:], T.ya[:]).then_inc(S["st"], 16)
    g.sync.wait_ge(S["st"], 16 * (N + 2))
